import numpy as np
import ml_dtypes


def mxq(x, axis, fmt="e4m3"):
    dtype, down = {"e4m3": (ml_dtypes.float8_e4m3fn, 7), "e5m2": (ml_dtypes.float8_e5m2, 14)}[fmt]
    v = np.moveaxis(np.asarray(x, np.float32).astype(ml_dtypes.bfloat16).astype(np.float64), axis, -1)
    blocks = v.reshape(v.shape[:-1] + (-1, 32))
    amax = np.abs(blocks).max(-1, keepdims=True)
    byte = np.maximum(np.where(amax > 0, np.frexp(amax)[1] - 1 + 127, 0) - down, 1)
    scale = np.exp2(byte - 127.0)
    codes = (blocks / scale).astype(np.float32).astype(dtype).astype(np.float64)
    return np.moveaxis((codes * scale).reshape(v.shape), -1, axis)


WIDE = False


def mx_kscale(k):
    if not WIDE:
        return np.ones(k)
    levels = np.array([10, -10, 5, -5, 0])
    if k % 512:
        return np.exp2(np.random.permutation(np.resize(levels, k // 32))).repeat(32)
    a = np.empty((k // 512, 16))
    for p in range(k // 512):
        a[p, :8] = np.random.permutation(np.resize(levels, 8))
        for g in range(8):
            far = levels[np.abs(levels - a[p, g]) >= 10]
            a[p, g + 8] = far[np.random.randint(len(far))]
    return np.exp2(a.ravel()).repeat(32)


def f64(x):
    return np.asarray(x).astype(np.float64)


def striped(idx):
    return np.tile(idx.reshape(-1, 16).T, (8, 1)).astype(np.uint16)


def unstriped(offs):
    return offs[:16].T.reshape(-1).astype(np.int64)


E2M1 = np.array([0.0, 0.5, 1.0, 1.5, 2.0, 3.0, 4.0, 6.0, -0.0, -0.5, -1.0, -1.5, -2.0, -3.0, -4.0, -6.0])


def pack_weight(w, fmt):
    k, n = w.shape
    w = f64(np.asarray(w, np.float32).astype(ml_dtypes.bfloat16)).reshape(k // 32, 32, n)
    amax = np.abs(w).max(1)
    if fmt == "e4m3":
        byte = np.frexp(amax)[1] - 1 + 127 - 7
    else:
        mant, ex = np.frexp(amax / 6.0)
        byte = np.where(mant > 0.5, ex, ex - 1) + 127
    byte = np.clip(np.where(amax > 0, byte, 1), 1, 254)
    scaled = (w * np.exp2(127.0 - byte)[:, None, :]).reshape(k, n).astype(np.float32)
    by_word = np.ascontiguousarray(scaled.reshape(k // 512, 128, 4, n).transpose(0, 1, 3, 2))
    if fmt == "e4m3":
        words = by_word.astype(ml_dtypes.float8_e4m3fn).view(np.uint8)
    else:
        c = by_word.astype(ml_dtypes.float4_e2m1fn).view(np.uint8) & 0xF
        words = (c[..., 0::2] | (c[..., 1::2] << 4)).reshape(k // 512, 128, 2 * n)
    return np.ascontiguousarray(words), np.ascontiguousarray(byte.astype(np.uint8).reshape(k // 512, 16, n))


def unpack_weight(words, scales, fmt):
    g, _, n = scales.shape
    words = np.ascontiguousarray(words).reshape(g, 128, n, -1)
    if fmt == "e4m3":
        vals = words.view(ml_dtypes.float8_e4m3fn).astype(np.float64)
    else:
        nib = np.empty((g, 128, n, 4), np.uint8)
        nib[..., 0::2] = words & 0xF
        nib[..., 1::2] = words >> 4
        vals = E2M1[nib]
    vals = vals * np.repeat(np.exp2(scales.astype(np.float64) - 127.0), 8, axis=1)[..., None]
    return vals.transpose(0, 1, 3, 2).reshape(g * 512, n)


def d_silu(v):
    s = 1.0 / (1.0 + np.exp(-np.maximum(v, -700.0)))
    return s * (1.0 + v * (1.0 - s))


K, T, E, C, H, N = 512, 768, 3, 256, 512, 512


def by_expert(wq, xq):
    return np.concatenate([wq[e].T @ xq[:, e * C:(e + 1) * C] for e in range(E)], axis=1)


def setup_inputs():
    n = np.random.standard_normal
    v = mx_kscale(N)
    u = mx_kscale(H)
    slot_token = np.random.permutation(T)[:E * C]
    w_slot = np.random.uniform(0.2, 1.0, E * C)
    partner = np.random.permutation(T)[:E * C]
    dy = pack_weight(n((N, T)) * v[:, None], "e4m3")
    wpt = [pack_weight(m, "e4m3") for m in n((E, H, K)) / np.sqrt(H) / u[None, :, None]]
    return {
        "dy_words": dy[0],
        "dy_scales": dy[1],
        "w2t": (n((E, N, H)) / np.sqrt(N) / v[None, :, None] * u).astype(np.float32),
        "w1t": (n((E, H, K)) / np.sqrt(H) / u[None, :, None]).astype(np.float32),
        "wpt_words": np.stack([m[0] for m in wpt]),
        "wpt_scales": np.stack([m[1] for m in wpt]),
        "a": (n((H, E * C))).astype(np.float32),
        "gate": (np.tile(w_slot, (128, 1))).astype(np.float32),
        "offs": striped(slot_token),
        "offs2": striped(partner),
    }


def reference(dy_words, dy_scales, w2t, w1t, wpt_words, wpt_scales, a, gate, offs, offs2):
    w2tq = mxq(f64(w2t), 1, "e4m3")
    w1tq = mxq(f64(w1t), 1, "e4m3")
    wpt = np.stack([unpack_weight(wpt_words[e], wpt_scales[e], "e4m3") for e in range(E)])
    idx, idx2 = unstriped(offs), unstriped(offs2)
    gq = unpack_weight(dy_words, dy_scales, "e4m3")[:, idx]
    dh = f64(gate[:1]) * by_expert(w2tq, gq) * d_silu(f64(a))
    dq = mxq(dh, 0, "e4m3")
    out = np.zeros((K, T))
    out[:, idx] = by_expert(w1tq, dq)
    out[:, idx2] += by_expert(wpt, dq)
    return out

@@ -1,0 +1,212 @@
+from contextlib import ExitStack
+
+import concourse.mybir as mybir
+
+K, T, E, C, H, N = 512, 768, 3, 256, 512, 512
+FLOPS = 3 * 2 * 512 * 512 * 768
+
+F32 = mybir.dt.float32
+BF16 = mybir.dt.bfloat16
+I32 = mybir.dt.int32
+U32 = mybir.dt.uint32
+U16 = mybir.dt.uint16
+U8 = mybir.dt.uint8
+FP8X4 = mybir.dt.float8_e4m3fn_x4
+ALU = mybir.AluOpType
+ACT = mybir.ActivationFunctionType
+
+P = 128
+PACK = 4
+HALF = 128
+LIST_COLS = C // 16
+
+
+def tile_moe_dub_silu_kernel(
+    tc, dy_words, dy_scales, w2t, w1t, wpt_words, wpt_scales, a, gate, offs, offs2, out
+):
+    nc = tc.nc
+    with ExitStack() as ctx:
+        lists = ctx.enter_context(tc.tile_pool(name="lists", bufs=1))
+        keep = ctx.enter_context(tc.tile_pool(name="keep", bufs=1))
+        psum = ctx.enter_context(tc.psum_pool(name="psum", bufs=1))
+
+        def sb(name, shape, dtype, tag=None, bufs=1):
+            return keep.tile(shape, dtype, name=name, tag=tag or name, bufs=bufs, align_bytes=64)
+
+        token_list = lists.tile([P, T // 16], U16, name="token_list")
+        partner_list = lists.tile([P, T // 16], U16, name="partner_list")
+
+        a_rows = a.rearrange("(p t) s -> p t s", t=PACK)
+        a_raw = [sb(f"a_raw{e}", [P, PACK, C], F32) for e in range(E)]
+        g = [sb(f"g{e}", [P, C], F32) for e in range(E)]
+        w2_raw = [sb(f"w2_raw{e}", [P, PACK, H], F32) for e in range(E)]
+        w1_raw = [sb(f"w1_raw{e}", [P, PACK, K], F32) for e in range(E)]
+        wp_words = [sb(f"wp_words{e}", [P, K], I32) for e in range(E)]
+        wp_scales = sb("wp_scales", [P, E, K], U8)
+        dyw = sb("dyw", [P, T], I32)
+        dys = sb("dys", [P, T], U8)
+
+        def load_a(e):
+            nc.sync.dma_start(out=a_raw[e][:], in_=a_rows[:, :, e * C:(e + 1) * C])
+            nc.sync.dma_start(out=g[e][:], in_=gate[:, e * C:(e + 1) * C])
+
+        def load_w(raw, w):
+            nc.sync.dma_start(out=raw[:], in_=w.rearrange("(p j) c -> p j c", j=PACK))
+
+        def load_wp(e):
+            nc.sync.dma_start(out=wp_words[e][:], in_=wpt_words[e, 0].rearrange("p k d -> p (k d)").bitcast(I32))
+
+        nc.gpsimd.memset(wp_scales[:].rearrange("p e k -> p (e k)").bitcast(I32), 0)
+
+        load_a(0)
+        nc.sync.dma_start(token_list[:], offs)
+        for q in range(4):
+            rows = dy_scales[0, 4 * q:4 * q + 4, :].bitcast(I32)
+            nc.sync.dma_start(out=dys[32 * q:32 * (q + 1), :].bitcast(I32),
+                              in_=rows.unsqueeze(0).to_broadcast([8, 4, T // 4]))
+        nc.sync.dma_start(out=dyw[:], in_=dy_words[0].rearrange("p t d -> p (t d)").bitcast(I32))
+        load_w(w2_raw[0], w2t[0])
+        load_wp(0)
+        for r in range(4):
+            nc.sync.dma_start(out=wp_scales[r:P:32, :, :].bitcast(I32),
+                              in_=wpt_scales[:, 0, r:16:4, :].rearrange("e q k -> q e k").bitcast(I32))
+        nc.sync.dma_start(partner_list[:], offs2)
+        load_w(w1_raw[0], w1t[0])
+        for e in range(1, E):
+            load_a(e)
+            load_w(w2_raw[e], w2t[e])
+            load_wp(e)
+            load_w(w1_raw[e], w1t[e])
+
+        gw = sb("gw", [P, T], I32)
+        gs = sb("gs", [P, T], U8)
+        for lo, hi in ((0, C), (C, T)):
+            part = token_list[:, lo // 16:hi // 16]
+            nc.vector.tensor_copy(gw[:, lo:hi].bitcast(U32), dyw[:].bitcast(U32).indirect(part))
+            nc.vector.tensor_copy(gs[:, lo:hi], dys[:].indirect(part))
+
+        def quantize(name, grouped, width):
+            codes = sb(name + "_codes", [P, width], U32)
+            scales = sb(name + "_scales", [P, width], U8)
+            nc.vector.quantize_mx(out=codes[:].bitcast(FP8X4), scales=scales[:], in_=grouped[:])
+            return codes, scales
+
+        def quantize_w2(e):
+            grouped = sb(f"w2_bf{e}", [P, PACK * H], BF16)
+            nc.scalar.copy(out=grouped[:].rearrange("p (t m j) -> p m j t", t=PACK, j=PACK),
+                           in_=w2_raw[e][:].rearrange("p j (m t) -> p m j t", t=PACK))
+            return quantize(f"w2_{e}", grouped, H)
+
+        def quantize_w1(e):
+            grouped = sb(f"w1_bf{e}", [P, PACK * K], BF16, tag="w1_bf", bufs=2)
+            nc.scalar.copy(out=grouped[:].rearrange("p (c i j) -> p c j i", i=4, j=PACK),
+                           in_=w1_raw[e][:].rearrange("p j (c i) -> p c j i", i=4))
+            return quantize(f"w1_{e}", grouped, K)
+
+        def activation(e, func, scale, name):
+            res = sb(f"{name}{e}", [P, C * PACK], F32, tag=name, bufs=2)
+            nc.scalar.activation(out=res[:].rearrange("p (c i t) -> p c t i", i=4, t=PACK),
+                                 in_=a_raw[e][:].rearrange("p t (c i) -> p c t i", i=4),
+                                 func=func, scale=scale)
+            return res
+
+        def factor(e):
+            order = [(ACT.Sigmoid, 1.0, "sig"), (ACT.Silu, -1.0, "nsilu")]
+            made = {}
+            for func, scale, name in (order if e % 2 == 0 else order[::-1]):
+                made[name] = activation(e, func, scale, name)
+            sg = sb(f"sg{e}", [P, C * PACK], F32, tag="sg", bufs=2)
+            z = sb(f"z{e}", [P, C * PACK], F32, tag="z", bufs=2)
+            for h in range(2):
+                cols = slice(h * HALF * PACK, (h + 1) * HALF * PACK)
+                gb = g[e][:, h * HALF:(h + 1) * HALF].unsqueeze(2).to_broadcast([P, HALF, PACK])
+                nc.gpsimd.tensor_tensor(out=sg[:, cols].rearrange("p (s t) -> p s t", t=PACK),
+                                        in0=made["sig"][:, cols].rearrange("p (s t) -> p s t", t=PACK),
+                                        in1=gb, op=ALU.mult)
+            nc.vector.scalar_tensor_tensor(out=z[:], in0=made["nsilu"][:], scalar=-1.0, in1=sg[:],
+                                           op0=ALU.add, op1=ALU.mult)
+            return z
+
+        def hidden(e, w2q, z):
+            codes, scales = w2q
+            dh = sb(f"dh{e}", [P, C * PACK], BF16)
+            for h in range(2):
+                bank = psum.tile([P, PACK, HALF], F32, name=f"s1_{e}_{h}", tag=f"s1_{h}")
+                slots = slice(e * C + h * HALF, e * C + (h + 1) * HALF)
+                for t in range(PACK):
+                    m = slice(t * P, (t + 1) * P)
+                    nc.tensor.matmul_mx(out=bank[:, t, :], lhsT=codes[:, m].bitcast(FP8X4), lhsT_scale=scales[:, m],
+                                        rhs=gw[:, slots].bitcast(FP8X4), rhs_scale=gs[:, slots], start=True, stop=True)
+                cols = slice(h * HALF * PACK, (h + 1) * HALF * PACK)
+                nc.vector.scalar_tensor_tensor(out=dh[:, cols].rearrange("p (s t) -> p s t", t=PACK),
+                                               in0=bank[:].rearrange("p t s -> p s t"), scalar=-1.0,
+                                               in1=z[:, cols].rearrange("p (s t) -> p s t", t=PACK),
+                                               op0=ALU.mult, op1=ALU.mult)
+            return quantize(f"dh_{e}", dh, C)
+
+        def products(label, jobs, dq):
+            staged = {}
+            for pair in range(len(jobs) // 2):
+                bank = psum.tile([P, 2, C], F32, name=f"s2_{label}_{pair}", tag="s2", bufs=4)
+                st = sb(f"st_{label}_{pair}", [P, 2, C], F32)
+                for u in range(2):
+                    name, kb, codes, scales = jobs[2 * pair + u]
+                    m = slice(kb * P, (kb + 1) * P)
+                    nc.tensor.matmul_mx(out=bank[:, u, :], lhsT=codes[:, m].bitcast(FP8X4), lhsT_scale=scales[:, m],
+                                        rhs=dq[0][:].bitcast(FP8X4), rhs_scale=dq[1][:], start=True, stop=True)
+                    staged[name, kb] = st[:, u, :]
+                nc.scalar.copy(out=st[:], in_=bank[:])
+            return staged
+
+        win = {}
+        index = {"dp": partner_list, "dx": token_list}
+
+        def scatter(e, name, kb, values, tag=None):
+            if (name, kb) not in win:
+                win[name, kb] = sb(f"win_{name}{kb}", [P, T], F32, tag=tag)
+            part = index[name][:, e * LIST_COLS:(e + 1) * LIST_COLS]
+            nc.vector.tensor_copy(win[name, kb][:].indirect(part), values[name, kb])
+
+        def jobs_of(name, q):
+            return [(name, kb, q[0], q[1]) for kb in range(4)]
+
+        def wp(e):
+            return wp_words[e], wp_scales[:, e, :]
+
+        z = factor(0)
+        dq = hidden(0, quantize_w2(0), z)
+        dp0 = products("dp0", jobs_of("dp", wp(0)), dq)
+        for kb in range(4):
+            scatter(0, "dp", kb, dp0)
+        dx0 = products("dx0", jobs_of("dx", quantize_w1(0)), dq)
+
+        z = factor(1)
+        w2q = quantize_w2(1)
+        scatter(0, "dx", 0, dx0, tag="w2_bf1")
+        dq = hidden(1, w2q, z)
+        scatter(0, "dx", 1, dx0, tag="dh1")
+        w1q = quantize_w1(1)
+        dp1 = products("dp1", jobs_of("dp", wp(1)), dq)
+        dx1 = products("dx1", jobs_of("dx", w1q), dq)
+        for kb in range(4):
+            scatter(1, "dp", kb, dp1)
+        for kb in range(2):
+            scatter(1, "dx", kb, dx1)
+
+        z = factor(2)
+        w2q = quantize_w2(2)
+        scatter(0, "dx", 2, dx0, tag="w2_bf2")
+        dq = hidden(2, w2q, z)
+        scatter(0, "dx", 3, dx0, tag="dh2")
+        w1q = quantize_w1(2)
+        jobs = [job for both in zip(jobs_of("dp", wp(2)), jobs_of("dx", w1q)) for job in both]
+        last = products("e2", jobs, dq)
+        for kb in range(2, 4):
+            scatter(1, "dx", kb, dx1)
+        for kb in range(4):
+            for name in ("dp", "dx"):
+                scatter(2, name, kb, last)
+            res = sb(f"res{kb}", [P, T], F32)
+            eng = nc.vector if kb == 3 else nc.gpsimd
+            eng.tensor_tensor(out=res[:], in0=win["dp", kb][:], in1=win["dx", kb][:], op=ALU.add)
+            nc.sync.dma_start(out=out[kb * P:(kb + 1) * P, :], in_=res[:])

@@ -58,13 +58,13 @@ def tile_moe_dub_silu_kernel(
 
         nc.gpsimd.memset(wp_scales[:].rearrange("p e k -> p (e k)").bitcast(I32), 0)
 
-        load_a(0)
         nc.sync.dma_start(token_list[:], offs)
+        nc.sync.dma_start(out=dyw[:], in_=dy_words[0].rearrange("p t d -> p (t d)").bitcast(I32))
         for q in range(4):
             rows = dy_scales[0, 4 * q:4 * q + 4, :].bitcast(I32)
             nc.sync.dma_start(out=dys[32 * q:32 * (q + 1), :].bitcast(I32),
                               in_=rows.unsqueeze(0).to_broadcast([8, 4, T // 4]))
-        nc.sync.dma_start(out=dyw[:], in_=dy_words[0].rearrange("p t d -> p (t d)").bitcast(I32))
+        load_a(0)
         load_w(w2_raw[0], w2t[0])
         load_wp(0)
         for r in range(4):
@@ -85,23 +85,32 @@ def tile_moe_dub_silu_kernel(
             nc.vector.tensor_copy(gw[:, lo:hi].bitcast(U32), dyw[:].bitcast(U32).indirect(part))
             nc.vector.tensor_copy(gs[:, lo:hi], dys[:].indirect(part))
 
-        def quantize(name, grouped, width):
+        def quantize(name, parts):
+            step = parts[0].shape[-1] // PACK
+            width = step * len(parts)
             codes = sb(name + "_codes", [P, width], U32)
             scales = sb(name + "_scales", [P, width], U8)
-            nc.vector.quantize_mx(out=codes[:].bitcast(FP8X4), scales=scales[:], in_=grouped[:])
+            for n, part in enumerate(parts):
+                cols = slice(n * step, (n + 1) * step)
+                nc.vector.quantize_mx(out=codes[:, cols].bitcast(FP8X4), scales=scales[:, cols], in_=part)
             return codes, scales
 
         def quantize_w2(e):
-            grouped = sb(f"w2_bf{e}", [P, PACK * H], BF16)
-            nc.scalar.copy(out=grouped[:].rearrange("p (t m j) -> p m j t", t=PACK, j=PACK),
-                           in_=w2_raw[e][:].rearrange("p j (m t) -> p m j t", t=PACK))
-            return quantize(f"w2_{e}", grouped, H)
+            grouped = sb(f"w2_bf{e}", [P, PACK * H], BF16, tag="w_bf", bufs=3)
+            dst = grouped[:].rearrange("p (t m j) -> p m j t", t=PACK, j=PACK)
+            src = w2_raw[e][:].rearrange("p j (m t) -> p m j t", t=PACK)
+            if e > 0:
+                nc.scalar.copy(out=dst, in_=src)
+                return quantize(f"w2_{e}", [grouped[:]])
+            for t in (0, 2):
+                nc.vector.tensor_copy(out=dst[:, :, :, t:t + 2], in_=src[:, :, :, t:t + 2])
+            return quantize(f"w2_{e}", [grouped[:, :2 * H], grouped[:, 2 * H:]])
 
         def quantize_w1(e):
-            grouped = sb(f"w1_bf{e}", [P, PACK * K], BF16, tag="w1_bf", bufs=2)
+            grouped = sb(f"w1_bf{e}", [P, PACK * K], BF16, tag="w_bf", bufs=3)
             nc.scalar.copy(out=grouped[:].rearrange("p (c i j) -> p c j i", i=4, j=PACK),
                            in_=w1_raw[e][:].rearrange("p j (c i) -> p c j i", i=4))
-            return quantize(f"w1_{e}", grouped, K)
+            return quantize(f"w1_{e}", [grouped[:]])
 
         def activation(e, func, scale, name):
             res = sb(f"{name}{e}", [P, C * PACK], F32, tag=name, bufs=2)
@@ -110,26 +119,49 @@ def tile_moe_dub_silu_kernel(
                                  func=func, scale=scale)
             return res
 
-        def factor(e):
-            order = [(ACT.Sigmoid, 1.0, "sig"), (ACT.Silu, -1.0, "nsilu")]
-            made = {}
-            for func, scale, name in (order if e % 2 == 0 else order[::-1]):
-                made[name] = activation(e, func, scale, name)
-            sg = sb(f"sg{e}", [P, C * PACK], F32, tag="sg", bufs=2)
-            z = sb(f"z{e}", [P, C * PACK], F32, tag="z", bufs=2)
+        def times_gate(e, dst, src, engines):
+            step = C // len(engines)
+            for n, eng in enumerate(engines):
+                cols = slice(n * step * PACK, (n + 1) * step * PACK)
+                gb = g[e][:, n * step:(n + 1) * step].unsqueeze(2).to_broadcast([P, step, PACK])
+                eng.tensor_tensor(out=dst[:, cols].rearrange("p (s t) -> p s t", t=PACK),
+                                  in0=src[:, cols].rearrange("p (s t) -> p s t", t=PACK),
+                                  in1=gb, op=ALU.mult)
+
+        def minus_one(tile):
             for h in range(2):
-                cols = slice(h * HALF * PACK, (h + 1) * HALF * PACK)
-                gb = g[e][:, h * HALF:(h + 1) * HALF].unsqueeze(2).to_broadcast([P, HALF, PACK])
-                nc.gpsimd.tensor_tensor(out=sg[:, cols].rearrange("p (s t) -> p s t", t=PACK),
-                                        in0=made["sig"][:, cols].rearrange("p (s t) -> p s t", t=PACK),
-                                        in1=gb, op=ALU.mult)
-            nc.vector.scalar_tensor_tensor(out=z[:], in0=made["nsilu"][:], scalar=-1.0, in1=sg[:],
-                                           op0=ALU.add, op1=ALU.mult)
+                half = tile[:, h * HALF * PACK:(h + 1) * HALF * PACK]
+                nc.gpsimd.tensor_scalar(out=half, in0=half, scalar1=1.0, scalar2=-1.0, op0=ALU.mult, op1=ALU.add)
+
+        def factor(e):
+            gated = sb(f"gated{e}", [P, C * PACK], F32, tag="gated", bufs=2)
+            z = [sb(f"z{e}_{h}", [P, HALF * PACK], F32, tag="z", bufs=4) for h in range(2)]
+            if e % 2 == 0:
+                sig = activation(e, ACT.Sigmoid, 1.0, "sig")
+                times_gate(e, gated, sig, [nc.gpsimd, nc.vector] if e == 0 else [nc.gpsimd] * 4)
+                other = activation(e, ACT.Silu, -1.0, "nsilu")
+                if e == 0:
+                    for h in range(2):
+                        cols = slice(h * HALF * PACK, (h + 1) * HALF * PACK)
+                        nc.vector.scalar_tensor_tensor(out=z[h][:], in0=other[:, cols], scalar=-1.0, in1=gated[:, cols],
+                                                       op0=ALU.add, op1=ALU.mult)
+                    return z
+                minus_one(other)
+            else:
+                nsilu = activation(e, ACT.Silu, -1.0, "nsilu")
+                minus_one(nsilu)
+                times_gate(e, gated, nsilu, [nc.gpsimd] * 4)
+                other = activation(e, ACT.Sigmoid, 1.0, "sig")
+            quarter = C * PACK // 4
+            for n in range(4):
+                cols = slice(n * quarter, (n + 1) * quarter)
+                nc.gpsimd.tensor_tensor(out=z[n // 2][:, (n % 2) * quarter:(n % 2 + 1) * quarter],
+                                        in0=other[:, cols], in1=gated[:, cols], op=ALU.mult)
             return z
 
         def hidden(e, w2q, z):
             codes, scales = w2q
-            dh = sb(f"dh{e}", [P, C * PACK], BF16)
+            dh = [sb(f"dh{e}_{h}", [P, HALF * PACK], BF16) for h in range(2)]
             for h in range(2):
                 bank = psum.tile([P, PACK, HALF], F32, name=f"s1_{e}_{h}", tag=f"s1_{h}")
                 slots = slice(e * C + h * HALF, e * C + (h + 1) * HALF)
@@ -137,76 +169,92 @@ def tile_moe_dub_silu_kernel(
                     m = slice(t * P, (t + 1) * P)
                     nc.tensor.matmul_mx(out=bank[:, t, :], lhsT=codes[:, m].bitcast(FP8X4), lhsT_scale=scales[:, m],
                                         rhs=gw[:, slots].bitcast(FP8X4), rhs_scale=gs[:, slots], start=True, stop=True)
-                cols = slice(h * HALF * PACK, (h + 1) * HALF * PACK)
-                nc.vector.scalar_tensor_tensor(out=dh[:, cols].rearrange("p (s t) -> p s t", t=PACK),
+                nc.vector.scalar_tensor_tensor(out=dh[h][:].rearrange("p (s t) -> p s t", t=PACK),
                                                in0=bank[:].rearrange("p t s -> p s t"), scalar=-1.0,
-                                               in1=z[:, cols].rearrange("p (s t) -> p s t", t=PACK),
+                                               in1=z[h][:].rearrange("p (s t) -> p s t", t=PACK),
                                                op0=ALU.mult, op1=ALU.mult)
-            return quantize(f"dh_{e}", dh, C)
+            return quantize(f"dh_{e}", [dh[0][:], dh[1][:]])
 
-        def products(label, jobs, dq):
-            staged = {}
-            for pair in range(len(jobs) // 2):
-                bank = psum.tile([P, 2, C], F32, name=f"s2_{label}_{pair}", tag="s2", bufs=4)
-                st = sb(f"st_{label}_{pair}", [P, 2, C], F32)
-                for u in range(2):
-                    name, kb, codes, scales = jobs[2 * pair + u]
-                    m = slice(kb * P, (kb + 1) * P)
-                    nc.tensor.matmul_mx(out=bank[:, u, :], lhsT=codes[:, m].bitcast(FP8X4), lhsT_scale=scales[:, m],
-                                        rhs=dq[0][:].bitcast(FP8X4), rhs_scale=dq[1][:], start=True, stop=True)
-                    staged[name, kb] = st[:, u, :]
-                nc.scalar.copy(out=st[:], in_=bank[:])
-            return staged
+        def bank_of(label, jobs, dq):
+            bank = psum.tile([P, 2, C], F32, name=f"s2_{label}", tag="s2", bufs=6)
+            for u, (kb, w) in enumerate(jobs):
+                m = slice(kb * P, (kb + 1) * P)
+                nc.tensor.matmul_mx(out=bank[:, u, :], lhsT=w[0][:, m].bitcast(FP8X4), lhsT_scale=w[1][:, m],
+                                    rhs=dq[0][:].bitcast(FP8X4), rhs_scale=dq[1][:], start=True, stop=True)
+            return bank
+
+        def staged(label, jobs, dq, tag=None):
+            st = sb(f"st_{label}", [P, 2, C], F32, tag=tag)
+            nc.scalar.copy(out=st[:], in_=bank_of(label, jobs, dq)[:])
+            return st
 
         win = {}
         index = {"dp": partner_list, "dx": token_list}
 
-        def scatter(e, name, kb, values, tag=None):
-            if (name, kb) not in win:
-                win[name, kb] = sb(f"win_{name}{kb}", [P, T], F32, tag=tag)
-            part = index[name][:, e * LIST_COLS:(e + 1) * LIST_COLS]
-            nc.vector.tensor_copy(win[name, kb][:].indirect(part), values[name, kb])
+        def scatter(first, name, kb, values):
+            count = values.shape[-1] // C
+            part = index[name][:, first * LIST_COLS:(first + count) * LIST_COLS]
+            nc.vector.tensor_copy(win[name, kb][:].indirect(part), values)
 
-        def jobs_of(name, q):
-            return [(name, kb, q[0], q[1]) for kb in range(4)]
+        def window(name, kb, tag=None):
+            win[name, kb] = sb(f"win_{name}{kb}", [P, T], F32, tag=tag)
 
         def wp(e):
             return wp_words[e], wp_scales[:, e, :]
 
         z = factor(0)
-        dq = hidden(0, quantize_w2(0), z)
-        dp0 = products("dp0", jobs_of("dp", wp(0)), dq)
+        dq0 = hidden(0, quantize_w2(0), z)
+        w1q0 = quantize_w1(0)
+        bank = bank_of("dp0_0", [(0, wp(0)), (1, wp(0))], dq0)
+        low = sb("st_dp0_0", [P, 2, C], F32)
+        for u in range(2):
+            nc.vector.tensor_copy(out=low[:, u, :], in_=bank[:, u, :])
+        high = staged("dp0_1", [(2, wp(0)), (3, wp(0))], dq0, tag="w1_raw0")
         for kb in range(4):
-            scatter(0, "dp", kb, dp0)
-        dx0 = products("dx0", jobs_of("dx", quantize_w1(0)), dq)
+            window("dp", kb)
+            scatter(0, "dp", kb, (low, high)[kb // 2][:, kb % 2, :])
 
         z = factor(1)
         w2q = quantize_w2(1)
-        scatter(0, "dx", 0, dx0, tag="w2_bf1")
-        dq = hidden(1, w2q, z)
-        scatter(0, "dx", 1, dx0, tag="dh1")
-        w1q = quantize_w1(1)
-        dp1 = products("dp1", jobs_of("dp", wp(1)), dq)
-        dx1 = products("dx1", jobs_of("dx", w1q), dq)
-        for kb in range(4):
-            scatter(1, "dp", kb, dp1)
+        dx0 = staged("dx0_0", [(0, w1q0), (1, w1q0)], dq0)
+        late = sb("st_late", [P, 2, 2 * C], F32)
+        nc.scalar.copy(out=late[:, :, 0:C], in_=bank_of("dx0_1", [(2, w1q0), (3, w1q0)], dq0)[:])
+        window("dx", 0)
+        scatter(0, "dx", 0, dx0[:, 0, :])
+        dq1 = hidden(1, w2q, z)
+        window("dx", 1, tag="dh1_0")
+        scatter(0, "dx", 1, dx0[:, 1, :])
+        w1q1 = quantize_w1(1)
+        for pair in range(2):
+            st = staged(f"dp1_{pair}", [(2 * pair, wp(1)), (2 * pair + 1, wp(1))], dq1)
+            for u in range(2):
+                scatter(1, "dp", 2 * pair + u, st[:, u, :])
+        dx1 = staged("dx1_0", [(0, w1q1), (1, w1q1)], dq1)
+        late_bank = bank_of("dx1_1", [(2, w1q1), (3, w1q1)], dq1)
         for kb in range(2):
-            scatter(1, "dx", kb, dx1)
+            scatter(1, "dx", kb, dx1[:, kb, :])
 
         z = factor(2)
         w2q = quantize_w2(2)
-        scatter(0, "dx", 2, dx0, tag="w2_bf2")
-        dq = hidden(2, w2q, z)
-        scatter(0, "dx", 3, dx0, tag="dh2")
-        w1q = quantize_w1(2)
-        jobs = [job for both in zip(jobs_of("dp", wp(2)), jobs_of("dx", w1q)) for job in both]
-        last = products("e2", jobs, dq)
-        for kb in range(2, 4):
-            scatter(1, "dx", kb, dx1)
+        nc.scalar.copy(out=late[:, 0, C:2 * C], in_=late_bank[:, 0, :])
+        window("dx", 2)
+        scatter(0, "dx", 2, late[:, 0, :])
+        dq2 = hidden(2, w2q, z)
+        w1q2 = quantize_w1(2)
+        nc.scalar.copy(out=late[:, 1, C:2 * C], in_=late_bank[:, 1, :])
+        window("dx", 3, tag="dh2_0")
+        scatter(0, "dx", 3, late[:, 1, :])
         for kb in range(4):
-            for name in ("dp", "dx"):
-                scatter(2, name, kb, last)
+            st = staged(f"e2_{kb}", [(kb, wp(2)), (kb, w1q2)], dq2)
+            scatter(2, "dp", kb, st[:, 0, :])
+            scatter(2, "dx", kb, st[:, 1, :])
             res = sb(f"res{kb}", [P, T], F32)
-            eng = nc.vector if kb == 3 else nc.gpsimd
-            eng.tensor_tensor(out=res[:], in0=win["dp", kb][:], in1=win["dx", kb][:], op=ALU.add)
-            nc.sync.dma_start(out=out[kb * P:(kb + 1) * P, :], in_=res[:])
+            rows = slice(kb * P, (kb + 1) * P)
+            if kb < 3:
+                nc.gpsimd.tensor_tensor(out=res[:], in0=win["dp", kb][:], in1=win["dx", kb][:], op=ALU.add)
+                nc.sync.dma_start(out=out[rows, :], in_=res[:])
+            else:
+                for queue, cols in ((nc.sync, slice(0, T // 2)), (nc.scalar, slice(T // 2, T))):
+                    nc.vector.tensor_tensor(out=res[:, cols], in0=win["dp", kb][:, cols], in1=win["dx", kb][:, cols],
+                                            op=ALU.add)
+                    queue.dma_start(out=out[rows, cols], in_=res[:, cols])

@@ -2,7 +2,7 @@ from contextlib import ExitStack
 
 import concourse.mybir as mybir
 
-K, T, E, C, H, N = 512, 768, 3, 256, 512, 512
+K, T, E, C, H = 512, 768, 3, 256, 512
 FLOPS = 3 * 2 * 512 * 512 * 768
 
 F32 = mybir.dt.float32
@@ -18,7 +18,11 @@ ACT = mybir.ActivationFunctionType
 P = 128
 PACK = 4
 HALF = 128
+HALF_COLS = HALF * PACK
 LIST_COLS = C // 16
+LINE = 4
+ROW_BLOCKS = K // P
+SHORT = 4
 
 
 def tile_moe_dub_silu_kernel(
@@ -71,12 +75,15 @@ def tile_moe_dub_silu_kernel(
             nc.sync.dma_start(out=wp_scales[r:P:32, :, :].bitcast(I32),
                               in_=wpt_scales[:, 0, r:16:4, :].rearrange("e q k -> q e k").bitcast(I32))
         nc.sync.dma_start(partner_list[:], offs2)
+        load_a(1)
         load_w(w1_raw[0], w1t[0])
-        for e in range(1, E):
-            load_a(e)
-            load_w(w2_raw[e], w2t[e])
-            load_wp(e)
-            load_w(w1_raw[e], w1t[e])
+        load_w(w2_raw[1], w2t[1])
+        load_wp(1)
+        load_w(w1_raw[1], w1t[1])
+        load_a(2)
+        load_w(w2_raw[2], w2t[2])
+        load_wp(2)
+        load_w(w1_raw[2], w1t[2])
 
         gw = sb("gw", [P, T], I32)
         gs = sb("gs", [P, T], U8)
@@ -96,7 +103,7 @@ def tile_moe_dub_silu_kernel(
             return codes, scales
 
         def quantize_w2(e):
-            grouped = sb(f"w2_bf{e}", [P, PACK * H], BF16, tag="w_bf", bufs=3)
+            grouped = sb(f"w2_bf{e}", [P, PACK * H], BF16, tag="w2_bf", bufs=2)
             dst = grouped[:].rearrange("p (t m j) -> p m j t", t=PACK, j=PACK)
             src = w2_raw[e][:].rearrange("p j (m t) -> p m j t", t=PACK)
             if e > 0:
@@ -107,17 +114,23 @@ def tile_moe_dub_silu_kernel(
             return quantize(f"w2_{e}", [grouped[:, :2 * H], grouped[:, 2 * H:]])
 
         def quantize_w1(e):
-            grouped = sb(f"w1_bf{e}", [P, PACK * K], BF16, tag="w_bf", bufs=3)
-            nc.scalar.copy(out=grouped[:].rearrange("p (c i j) -> p c j i", i=4, j=PACK),
-                           in_=w1_raw[e][:].rearrange("p j (c i) -> p c j i", i=4))
+            grouped = sb(f"w1_bf{e}", [P, PACK * K], BF16)
+            nc.scalar.copy(out=grouped[:].rearrange("p (c i j) -> p c j i", i=LINE, j=PACK),
+                           in_=w1_raw[e][:].rearrange("p j (c i) -> p c j i", i=LINE))
             return quantize(f"w1_{e}", [grouped[:]])
 
         def activation(e, func, scale, name):
             res = sb(f"{name}{e}", [P, C * PACK], F32, tag=name, bufs=2)
-            nc.scalar.activation(out=res[:].rearrange("p (c i t) -> p c t i", i=4, t=PACK),
-                                 in_=a_raw[e][:].rearrange("p t (c i) -> p c t i", i=4),
+            nc.scalar.activation(out=res[:].rearrange("p (c i t) -> p c t i", i=LINE, t=PACK),
+                                 in_=a_raw[e][:].rearrange("p t (c i) -> p c t i", i=LINE),
                                  func=func, scale=scale)
             return res
+
+        def sigmoid(e):
+            return activation(e, ACT.Sigmoid, 1.0, "sig")
+
+        def silu_of_minus(e):
+            return activation(e, ACT.Silu, -1.0, "nsilu")
 
         def times_gate(e, dst, src, engines):
             step = C // len(engines)
@@ -128,40 +141,51 @@ def tile_moe_dub_silu_kernel(
                                   in0=src[:, cols].rearrange("p (s t) -> p s t", t=PACK),
                                   in1=gb, op=ALU.mult)
 
-        def minus_one(tile):
+        def minus_one(dst, src):
             for h in range(2):
-                half = tile[:, h * HALF * PACK:(h + 1) * HALF * PACK]
-                nc.gpsimd.tensor_scalar(out=half, in0=half, scalar1=1.0, scalar2=-1.0, op0=ALU.mult, op1=ALU.add)
+                cols = slice(h * HALF_COLS, (h + 1) * HALF_COLS)
+                nc.gpsimd.tensor_scalar(out=dst[:, cols], in0=src[:, cols], scalar1=1.0, scalar2=-1.0,
+                                        op0=ALU.mult, op1=ALU.add)
 
-        def factor(e):
-            gated = sb(f"gated{e}", [P, C * PACK], F32, tag="gated", bufs=2)
-            z = [sb(f"z{e}_{h}", [P, HALF * PACK], F32, tag="z", bufs=4) for h in range(2)]
-            if e % 2 == 0:
-                sig = activation(e, ACT.Sigmoid, 1.0, "sig")
-                times_gate(e, gated, sig, [nc.gpsimd, nc.vector] if e == 0 else [nc.gpsimd] * 4)
-                other = activation(e, ACT.Silu, -1.0, "nsilu")
-                if e == 0:
-                    for h in range(2):
-                        cols = slice(h * HALF * PACK, (h + 1) * HALF * PACK)
-                        nc.vector.scalar_tensor_tensor(out=z[h][:], in0=other[:, cols], scalar=-1.0, in1=gated[:, cols],
-                                                       op0=ALU.add, op1=ALU.mult)
-                    return z
-                minus_one(other)
-            else:
-                nsilu = activation(e, ACT.Silu, -1.0, "nsilu")
-                minus_one(nsilu)
-                times_gate(e, gated, nsilu, [nc.gpsimd] * 4)
-                other = activation(e, ACT.Sigmoid, 1.0, "sig")
-            quarter = C * PACK // 4
-            for n in range(4):
-                cols = slice(n * quarter, (n + 1) * quarter)
-                nc.gpsimd.tensor_tensor(out=z[n // 2][:, (n % 2) * quarter:(n % 2 + 1) * quarter],
-                                        in0=other[:, cols], in1=gated[:, cols], op=ALU.mult)
+        def factor_tiles(e, gated_tag):
+            gated = sb(f"gated{e}", [P, C * PACK], F32, tag=gated_tag)
+            return gated, [sb(f"z{e}_{h}", [P, HALF_COLS], F32, tag="z", bufs=4) for h in range(2)]
+
+        def product_on_gpsimd(z, left, right):
+            step = C * PACK // SHORT
+            for n in range(SHORT):
+                cols = slice(n * step, (n + 1) * step)
+                nc.gpsimd.tensor_tensor(out=z[n // 2][:, (n % 2) * step:(n % 2 + 1) * step],
+                                        in0=left[:, cols], in1=right[:, cols], op=ALU.mult)
+
+        def factor_0():
+            gated, z = factor_tiles(0, None)
+            times_gate(0, gated, sigmoid(0), [nc.gpsimd, nc.vector])
+            nsilu = silu_of_minus(0)
+            for h in range(2):
+                cols = slice(h * HALF_COLS, (h + 1) * HALF_COLS)
+                nc.vector.scalar_tensor_tensor(out=z[h][:], in0=nsilu[:, cols], scalar=-1.0, in1=gated[:, cols],
+                                               op0=ALU.add, op1=ALU.mult)
+            return z
+
+        def factor_1():
+            gated, z = factor_tiles(1, "dh0_1")
+            minus_one(gated, silu_of_minus(1))
+            times_gate(1, gated, gated, [nc.gpsimd] * SHORT)
+            product_on_gpsimd(z, sigmoid(1), gated)
+            return z
+
+        def factor_2():
+            gated, z = factor_tiles(2, "w1_bf1")
+            times_gate(2, gated, sigmoid(2), [nc.gpsimd] * SHORT)
+            nsilu = silu_of_minus(2)
+            minus_one(nsilu, nsilu)
+            product_on_gpsimd(z, nsilu, gated)
             return z
 
         def hidden(e, w2q, z):
             codes, scales = w2q
-            dh = [sb(f"dh{e}_{h}", [P, HALF * PACK], BF16) for h in range(2)]
+            dh = [sb(f"dh{e}_{h}", [P, HALF_COLS], BF16) for h in range(2)]
             for h in range(2):
                 bank = psum.tile([P, PACK, HALF], F32, name=f"s1_{e}_{h}", tag=f"s1_{h}")
                 slots = slice(e * C + h * HALF, e * C + (h + 1) * HALF)
@@ -183,8 +207,8 @@ def tile_moe_dub_silu_kernel(
                                     rhs=dq[0][:].bitcast(FP8X4), rhs_scale=dq[1][:], start=True, stop=True)
             return bank
 
-        def staged(label, jobs, dq, tag=None):
-            st = sb(f"st_{label}", [P, 2, C], F32, tag=tag)
+        def staged(label, jobs, dq):
+            st = sb(f"st_{label}", [P, 2, C], F32)
             nc.scalar.copy(out=st[:], in_=bank_of(label, jobs, dq)[:])
             return st
 
@@ -202,19 +226,19 @@ def tile_moe_dub_silu_kernel(
         def wp(e):
             return wp_words[e], wp_scales[:, e, :]
 
-        z = factor(0)
+        z = factor_0()
         dq0 = hidden(0, quantize_w2(0), z)
-        w1q0 = quantize_w1(0)
         bank = bank_of("dp0_0", [(0, wp(0)), (1, wp(0))], dq0)
         low = sb("st_dp0_0", [P, 2, C], F32)
         for u in range(2):
             nc.vector.tensor_copy(out=low[:, u, :], in_=bank[:, u, :])
-        high = staged("dp0_1", [(2, wp(0)), (3, wp(0))], dq0, tag="w1_raw0")
-        for kb in range(4):
-            window("dp", kb)
+        z = factor_1()
+        high = staged("dp0_1", [(2, wp(0)), (3, wp(0))], dq0)
+        w1q0 = quantize_w1(0)
+        for kb in range(ROW_BLOCKS):
+            window("dp", kb, tag="w1_bf0" if kb == ROW_BLOCKS - 1 else None)
             scatter(0, "dp", kb, (low, high)[kb // 2][:, kb % 2, :])
 
-        z = factor(1)
         w2q = quantize_w2(1)
         dx0 = staged("dx0_0", [(0, w1q0), (1, w1q0)], dq0)
         late = sb("st_late", [P, 2, 2 * C], F32)
@@ -234,7 +258,7 @@ def tile_moe_dub_silu_kernel(
         for kb in range(2):
             scatter(1, "dx", kb, dx1[:, kb, :])
 
-        z = factor(2)
+        z = factor_2()
         w2q = quantize_w2(2)
         nc.scalar.copy(out=late[:, 0, C:2 * C], in_=late_bank[:, 0, :])
         window("dx", 2)
@@ -244,13 +268,14 @@ def tile_moe_dub_silu_kernel(
         nc.scalar.copy(out=late[:, 1, C:2 * C], in_=late_bank[:, 1, :])
         window("dx", 3, tag="dh2_0")
         scatter(0, "dx", 3, late[:, 1, :])
-        for kb in range(4):
+
+        for kb in range(ROW_BLOCKS):
             st = staged(f"e2_{kb}", [(kb, wp(2)), (kb, w1q2)], dq2)
             scatter(2, "dp", kb, st[:, 0, :])
             scatter(2, "dx", kb, st[:, 1, :])
             res = sb(f"res{kb}", [P, T], F32)
             rows = slice(kb * P, (kb + 1) * P)
-            if kb < 3:
+            if kb < ROW_BLOCKS - 1:
                 nc.gpsimd.tensor_tensor(out=res[:], in0=win["dp", kb][:], in1=win["dx", kb][:], op=ALU.add)
                 nc.sync.dma_start(out=out[rows, :], in_=res[:])
             else:

from contextlib import ExitStack

import concourse.mybir as mybir

K, T, E, C, H = 512, 768, 3, 256, 512
FLOPS = 3 * 2 * 512 * 512 * 768

F32 = mybir.dt.float32
BF16 = mybir.dt.bfloat16
I32 = mybir.dt.int32
U32 = mybir.dt.uint32
U16 = mybir.dt.uint16
U8 = mybir.dt.uint8
FP8X4 = mybir.dt.float8_e4m3fn_x4
ALU = mybir.AluOpType
ACT = mybir.ActivationFunctionType

P = 128
PACK = 4
HALF = 128
HALF_COLS = HALF * PACK
LIST_COLS = C // 16
LINE = 4
ROW_BLOCKS = K // P
SHORT = 4


def tile_moe_dub_silu_kernel(
    tc, dy_words, dy_scales, w2t, w1t, wpt_words, wpt_scales, a, gate, offs, offs2, out
):
    nc = tc.nc
    with ExitStack() as ctx:
        lists = ctx.enter_context(tc.tile_pool(name="lists", bufs=1))
        keep = ctx.enter_context(tc.tile_pool(name="keep", bufs=1))
        psum = ctx.enter_context(tc.psum_pool(name="psum", bufs=1))

        def sb(name, shape, dtype, tag=None, bufs=1):
            return keep.tile(shape, dtype, name=name, tag=tag or name, bufs=bufs, align_bytes=64)

        token_list = lists.tile([P, T // 16], U16, name="token_list")
        partner_list = lists.tile([P, T // 16], U16, name="partner_list")

        a_rows = a.rearrange("(p t) s -> p t s", t=PACK)
        a_raw = [sb(f"a_raw{e}", [P, PACK, C], F32) for e in range(E)]
        g = [sb(f"g{e}", [P, C], F32) for e in range(E)]
        w2_raw = [sb(f"w2_raw{e}", [P, PACK, H], F32) for e in range(E)]
        w1_raw = [sb(f"w1_raw{e}", [P, PACK, K], F32) for e in range(E)]
        wp_words = [sb(f"wp_words{e}", [P, K], I32) for e in range(E)]
        wp_scales = sb("wp_scales", [P, E, K], U8)
        dyw = sb("dyw", [P, T], I32)
        dys = sb("dys", [P, T], U8)

        def load_a(e):
            nc.sync.dma_start(out=a_raw[e][:], in_=a_rows[:, :, e * C:(e + 1) * C])
            nc.sync.dma_start(out=g[e][:], in_=gate[:, e * C:(e + 1) * C])

        def load_w(raw, w):
            nc.sync.dma_start(out=raw[:], in_=w.rearrange("(p j) c -> p j c", j=PACK))

        def load_wp(e):
            nc.sync.dma_start(out=wp_words[e][:], in_=wpt_words[e, 0].rearrange("p k d -> p (k d)").bitcast(I32))

        nc.gpsimd.memset(wp_scales[:].rearrange("p e k -> p (e k)").bitcast(I32), 0)

        nc.sync.dma_start(token_list[:], offs)
        nc.sync.dma_start(out=dyw[:], in_=dy_words[0].rearrange("p t d -> p (t d)").bitcast(I32))
        for q in range(4):
            rows = dy_scales[0, 4 * q:4 * q + 4, :].bitcast(I32)
            nc.sync.dma_start(out=dys[32 * q:32 * (q + 1), :].bitcast(I32),
                              in_=rows.unsqueeze(0).to_broadcast([8, 4, T // 4]))
        load_a(0)
        load_w(w2_raw[0], w2t[0])
        load_wp(0)
        for r in range(4):
            nc.sync.dma_start(out=wp_scales[r:P:32, :, :].bitcast(I32),
                              in_=wpt_scales[:, 0, r:16:4, :].rearrange("e q k -> q e k").bitcast(I32))
        nc.sync.dma_start(partner_list[:], offs2)
        load_a(1)
        load_w(w1_raw[0], w1t[0])
        load_w(w2_raw[1], w2t[1])
        load_wp(1)
        load_w(w1_raw[1], w1t[1])
        load_a(2)
        load_w(w2_raw[2], w2t[2])
        load_wp(2)
        load_w(w1_raw[2], w1t[2])

        gw = sb("gw", [P, T], I32)
        gs = sb("gs", [P, T], U8)
        for lo, hi in ((0, C), (C, T)):
            part = token_list[:, lo // 16:hi // 16]
            nc.vector.tensor_copy(gw[:, lo:hi].bitcast(U32), dyw[:].bitcast(U32).indirect(part))
            nc.vector.tensor_copy(gs[:, lo:hi], dys[:].indirect(part))

        def quantize(name, parts):
            step = parts[0].shape[-1] // PACK
            width = step * len(parts)
            codes = sb(name + "_codes", [P, width], U32)
            scales = sb(name + "_scales", [P, width], U8)
            for n, part in enumerate(parts):
                cols = slice(n * step, (n + 1) * step)
                nc.vector.quantize_mx(out=codes[:, cols].bitcast(FP8X4), scales=scales[:, cols], in_=part)
            return codes, scales

        def quantize_w2(e):
            grouped = sb(f"w2_bf{e}", [P, PACK * H], BF16, tag="w2_bf", bufs=2)
            dst = grouped[:].rearrange("p (t m j) -> p m j t", t=PACK, j=PACK)
            src = w2_raw[e][:].rearrange("p j (m t) -> p m j t", t=PACK)
            if e > 0:
                nc.scalar.copy(out=dst, in_=src)
                return quantize(f"w2_{e}", [grouped[:]])
            for t in (0, 2):
                nc.vector.tensor_copy(out=dst[:, :, :, t:t + 2], in_=src[:, :, :, t:t + 2])
            return quantize(f"w2_{e}", [grouped[:, :2 * H], grouped[:, 2 * H:]])

        def quantize_w1(e):
            grouped = sb(f"w1_bf{e}", [P, PACK * K], BF16)
            nc.scalar.copy(out=grouped[:].rearrange("p (c i j) -> p c j i", i=LINE, j=PACK),
                           in_=w1_raw[e][:].rearrange("p j (c i) -> p c j i", i=LINE))
            return quantize(f"w1_{e}", [grouped[:]])

        def activation(e, func, scale, name):
            res = sb(f"{name}{e}", [P, C * PACK], F32, tag=name, bufs=2)
            nc.scalar.activation(out=res[:].rearrange("p (c i t) -> p c t i", i=LINE, t=PACK),
                                 in_=a_raw[e][:].rearrange("p t (c i) -> p c t i", i=LINE),
                                 func=func, scale=scale)
            return res

        def sigmoid(e):
            return activation(e, ACT.Sigmoid, 1.0, "sig")

        def silu_of_minus(e):
            return activation(e, ACT.Silu, -1.0, "nsilu")

        def times_gate(e, dst, src, engines):
            step = C // len(engines)
            for n, eng in enumerate(engines):
                cols = slice(n * step * PACK, (n + 1) * step * PACK)
                gb = g[e][:, n * step:(n + 1) * step].unsqueeze(2).to_broadcast([P, step, PACK])
                eng.tensor_tensor(out=dst[:, cols].rearrange("p (s t) -> p s t", t=PACK),
                                  in0=src[:, cols].rearrange("p (s t) -> p s t", t=PACK),
                                  in1=gb, op=ALU.mult)

        def minus_one(dst, src):
            for h in range(2):
                cols = slice(h * HALF_COLS, (h + 1) * HALF_COLS)
                nc.gpsimd.tensor_scalar(out=dst[:, cols], in0=src[:, cols], scalar1=1.0, scalar2=-1.0,
                                        op0=ALU.mult, op1=ALU.add)

        def factor_tiles(e, gated_tag):
            gated = sb(f"gated{e}", [P, C * PACK], F32, tag=gated_tag)
            return gated, [sb(f"z{e}_{h}", [P, HALF_COLS], F32, tag="z", bufs=4) for h in range(2)]

        def product_on_gpsimd(z, left, right):
            step = C * PACK // SHORT
            for n in range(SHORT):
                cols = slice(n * step, (n + 1) * step)
                nc.gpsimd.tensor_tensor(out=z[n // 2][:, (n % 2) * step:(n % 2 + 1) * step],
                                        in0=left[:, cols], in1=right[:, cols], op=ALU.mult)

        def factor_0():
            gated, z = factor_tiles(0, None)
            times_gate(0, gated, sigmoid(0), [nc.gpsimd, nc.vector])
            nsilu = silu_of_minus(0)
            for h in range(2):
                cols = slice(h * HALF_COLS, (h + 1) * HALF_COLS)
                nc.vector.scalar_tensor_tensor(out=z[h][:], in0=nsilu[:, cols], scalar=-1.0, in1=gated[:, cols],
                                               op0=ALU.add, op1=ALU.mult)
            return z

        def factor_1():
            gated, z = factor_tiles(1, "dh0_1")
            minus_one(gated, silu_of_minus(1))
            times_gate(1, gated, gated, [nc.gpsimd] * SHORT)
            product_on_gpsimd(z, sigmoid(1), gated)
            return z

        def factor_2():
            gated, z = factor_tiles(2, "w1_bf1")
            times_gate(2, gated, sigmoid(2), [nc.gpsimd] * SHORT)
            nsilu = silu_of_minus(2)
            minus_one(nsilu, nsilu)
            product_on_gpsimd(z, nsilu, gated)
            return z

        def hidden(e, w2q, z):
            codes, scales = w2q
            dh = [sb(f"dh{e}_{h}", [P, HALF_COLS], BF16) for h in range(2)]
            for h in range(2):
                bank = psum.tile([P, PACK, HALF], F32, name=f"s1_{e}_{h}", tag=f"s1_{h}")
                slots = slice(e * C + h * HALF, e * C + (h + 1) * HALF)
                for t in range(PACK):
                    m = slice(t * P, (t + 1) * P)
                    nc.tensor.matmul_mx(out=bank[:, t, :], lhsT=codes[:, m].bitcast(FP8X4), lhsT_scale=scales[:, m],
                                        rhs=gw[:, slots].bitcast(FP8X4), rhs_scale=gs[:, slots], start=True, stop=True)
                nc.vector.scalar_tensor_tensor(out=dh[h][:].rearrange("p (s t) -> p s t", t=PACK),
                                               in0=bank[:].rearrange("p t s -> p s t"), scalar=-1.0,
                                               in1=z[h][:].rearrange("p (s t) -> p s t", t=PACK),
                                               op0=ALU.mult, op1=ALU.mult)
            return quantize(f"dh_{e}", [dh[0][:], dh[1][:]])

        def bank_of(label, jobs, dq):
            bank = psum.tile([P, 2, C], F32, name=f"s2_{label}", tag="s2", bufs=6)
            for u, (kb, w) in enumerate(jobs):
                m = slice(kb * P, (kb + 1) * P)
                nc.tensor.matmul_mx(out=bank[:, u, :], lhsT=w[0][:, m].bitcast(FP8X4), lhsT_scale=w[1][:, m],
                                    rhs=dq[0][:].bitcast(FP8X4), rhs_scale=dq[1][:], start=True, stop=True)
            return bank

        def staged(label, jobs, dq):
            st = sb(f"st_{label}", [P, 2, C], F32)
            nc.scalar.copy(out=st[:], in_=bank_of(label, jobs, dq)[:])
            return st

        win = {}
        index = {"dp": partner_list, "dx": token_list}

        def scatter(first, name, kb, values):
            count = values.shape[-1] // C
            part = index[name][:, first * LIST_COLS:(first + count) * LIST_COLS]
            nc.vector.tensor_copy(win[name, kb][:].indirect(part), values)

        def window(name, kb, tag=None):
            win[name, kb] = sb(f"win_{name}{kb}", [P, T], F32, tag=tag)

        def wp(e):
            return wp_words[e], wp_scales[:, e, :]

        z = factor_0()
        dq0 = hidden(0, quantize_w2(0), z)
        bank = bank_of("dp0_0", [(0, wp(0)), (1, wp(0))], dq0)
        low = sb("st_dp0_0", [P, 2, C], F32)
        for u in range(2):
            nc.vector.tensor_copy(out=low[:, u, :], in_=bank[:, u, :])
        z = factor_1()
        high = staged("dp0_1", [(2, wp(0)), (3, wp(0))], dq0)
        w1q0 = quantize_w1(0)
        for kb in range(ROW_BLOCKS):
            window("dp", kb, tag="w1_bf0" if kb == ROW_BLOCKS - 1 else None)
            scatter(0, "dp", kb, (low, high)[kb // 2][:, kb % 2, :])

        w2q = quantize_w2(1)
        dx0 = staged("dx0_0", [(0, w1q0), (1, w1q0)], dq0)
        late = sb("st_late", [P, 2, 2 * C], F32)
        nc.scalar.copy(out=late[:, :, 0:C], in_=bank_of("dx0_1", [(2, w1q0), (3, w1q0)], dq0)[:])
        window("dx", 0)
        scatter(0, "dx", 0, dx0[:, 0, :])
        dq1 = hidden(1, w2q, z)
        window("dx", 1, tag="dh1_0")
        scatter(0, "dx", 1, dx0[:, 1, :])
        w1q1 = quantize_w1(1)
        for pair in range(2):
            st = staged(f"dp1_{pair}", [(2 * pair, wp(1)), (2 * pair + 1, wp(1))], dq1)
            for u in range(2):
                scatter(1, "dp", 2 * pair + u, st[:, u, :])
        dx1 = staged("dx1_0", [(0, w1q1), (1, w1q1)], dq1)
        late_bank = bank_of("dx1_1", [(2, w1q1), (3, w1q1)], dq1)
        for kb in range(2):
            scatter(1, "dx", kb, dx1[:, kb, :])

        z = factor_2()
        w2q = quantize_w2(2)
        nc.scalar.copy(out=late[:, 0, C:2 * C], in_=late_bank[:, 0, :])
        window("dx", 2)
        scatter(0, "dx", 2, late[:, 0, :])
        dq2 = hidden(2, w2q, z)
        w1q2 = quantize_w1(2)
        nc.scalar.copy(out=late[:, 1, C:2 * C], in_=late_bank[:, 1, :])
        window("dx", 3, tag="dh2_0")
        scatter(0, "dx", 3, late[:, 1, :])

        for kb in range(ROW_BLOCKS):
            st = staged(f"e2_{kb}", [(kb, wp(2)), (kb, w1q2)], dq2)
            scatter(2, "dp", kb, st[:, 0, :])
            scatter(2, "dx", kb, st[:, 1, :])
            res = sb(f"res{kb}", [P, T], F32)
            rows = slice(kb * P, (kb + 1) * P)
            if kb < ROW_BLOCKS - 1:
                nc.gpsimd.tensor_tensor(out=res[:], in0=win["dp", kb][:], in1=win["dx", kb][:], op=ALU.add)
                nc.sync.dma_start(out=out[rows, :], in_=res[:])
            else:
                for queue, cols in ((nc.sync, slice(0, T // 2)), (nc.scalar, slice(T // 2, T))):
                    nc.vector.tensor_tensor(out=res[:, cols], in0=win["dp", kb][:, cols], in1=win["dx", kb][:, cols],
                                            op=ALU.add)
                    queue.dma_start(out=out[rows, cols], in_=res[:, cols])
